import numpy as np, ml_dtypes
CORES = [1,5,17,21,33,37,49,53]
N = 8
import mx_ref
BF = ml_dtypes.bfloat16
def entries(a):
    return np.ascontiguousarray(a.T).reshape(-1)
def table(e):
    return np.ascontiguousarray(np.reshape(e, (-1, 16)).T).astype(np.int32)
def cut(t, i, w=512):
    return t[:, w * i:w * i + w]
def f(rng, *shape):
    return mx_ref.flush((rng.standard_normal(shape, dtype=np.float32) * np.exp2(rng.integers(-2, 3, shape[:-1] + (1,)))).astype(BF))
def wide(rng, *shape, cols=0):
    v = rng.standard_normal(shape, dtype=np.float32) * np.exp2(rng.integers(-12, 13, shape)).astype(np.float32)
    if cols: v *= np.repeat(np.exp2(rng.integers(-cols, cols + 1, shape[:-2] + (1, shape[-1] // 4))) * (rng.random(shape[:-2] + (1, shape[-1] // 4)) > 0.0625), 4, axis=-1).astype(np.float32)
    return mx_ref.flush(v.astype(BF))
PG, NW, SP, CW, CP, O = 32, 64, 32, 16, 6, 2
def counts(rng, total, cap, least):
    n = np.array(least)
    while n.sum() < total: n[rng.choice(np.flatnonzero(n < cap))] += 1
    return n
def lists(rng, full=False, own=False, shared=False, rewritten=False):
    h = int(rng.integers(0, N)); hot = rng.permutation(PG)[:CP if shared else 2]
    fr, pg = np.zeros((N, SP), int), np.zeros((N, SP), int)
    rd, wr, wp = np.full((N, N * CP), -1), np.full((N, N * CW), -1), np.full((N, N * CW), -1)
    for s in range(N):
        lw, lp = np.zeros(N, int), np.zeros(N, int)
        if full:
            a = np.append(h, rng.permutation(np.delete(np.arange(N), h)))
            lw[a[:NW // CW]] = CW; lp[a[:SP // CP]] = CP
        if own: lw[s] = CW; lp[s] = CP
        if shared: lw[h] = CW; lp[h] = CP
        if rewritten: lw[h] = CW; lp[h] = 1
        n, fresh, at = counts(rng, NW, CW, lw), rng.permutation(NW), 0
        for q in range(N):
            c = rng.permutation(CW)[:n[q]]
            wr[s, q * CW + c] = fresh[at:at + n[q]]; wp[q, s * CW + c] = 0; at += n[q]
        n, slots, frames = counts(rng, SP, CP, lp), [], []
        for q in range(N):
            must = np.zeros(0, int)
            if q == h and shared: must = hot
            if q == h and rewritten: must = hot[s % 2:s % 2 + 1]
            g = np.concatenate([must, rng.permutation(np.setdiff1d(np.arange(PG), must))])[:n[q]]
            c = rng.permutation(CP)[:n[q]]
            rd[q, s * CP + c] = g; slots.append(q * CP + c); frames.append(q * PG + g)
        o = rng.permutation(SP)
        pg[s] = np.concatenate(slots)[o]; fr[s] = np.concatenate(frames)[o]
    for q in range(N):
        k = np.flatnonzero(wp[q] >= 0); must = np.zeros(0, int)
        if q == h and shared: must = 16 * hot + rng.integers(0, 16, hot.size)
        if q == h and rewritten: must = (16 * hot[:, None] + np.arange(16)).reshape(-1)
        p = np.concatenate([must, rng.permutation(np.setdiff1d(np.arange(16 * PG), must))])[:k.size]
        wp[q, k] = rng.permutation(p)
    return {n: np.stack([table(v) for v in a]) for n, a in (("fr", fr), ("wr", wr), ("wp", wp), ("rd", rd), ("pg", pg))}
def setup_inputs(rng):
    return {"pl": f(rng, N, 128, 64 * PG), "nw": f(rng, N, 128, 4 * NW), "qw": f(rng, N, 128, 512 * O), **lists(rng)}
def setup_inputs_full(rng):
    return {**setup_inputs(rng), **lists(rng, full=True)}
def setup_inputs_own(rng):
    return {**setup_inputs(rng), **lists(rng, own=True)}
def setup_inputs_rewritten(rng):
    return {**setup_inputs(rng), **lists(rng, rewritten=True)}
def setup_inputs_shared(rng):
    return {**setup_inputs(rng), **lists(rng, shared=True)}
def setup_inputs_spread(rng):
    d = setup_inputs(rng); d["pl"] = wide(rng, N, 128, 64 * PG, cols=8); d["nw"] = wide(rng, N, 128, 4 * NW, cols=8); return d
def check_inputs(d):
    b = []
    for r in range(N):
        t, a, p, k, g = [entries(d[n][r]) for n in ("fr", "wr", "wp", "rd", "pg")]
        if t.min() < 0 or t.max() >= N * PG or len(set(t.tolist())) != SP: b.append("fr")
        if a.min() < -1 or a.max() >= NW or sorted(a[a >= 0].tolist()) != list(range(NW)): b.append("wr")
        sent = np.concatenate([entries(d["wr"][s])[r * CW:r * CW + CW] for s in range(N)]); v = p[p >= 0]
        if p.min() < -1 or p.max() >= 16 * PG or len(set(v.tolist())) != v.size or ((p >= 0) != (sent >= 0)).any(): b.append("wp")
        if k.min() < -1 or k.max() >= PG: b.append("rd")
        got = np.concatenate([entries(d["rd"][q])[r * CP:r * CP + CP] for q in range(N)])
        if g.min() < 0 or g.max() >= N * CP or len(set(g.tolist())) != SP or (got >= 0).sum() != SP: b.append("pg")
        elif (got[g] < 0).any() or (g // CP * PG + got[g] != t).any(): b.append("pg")
    return b
def reference(pl, nw, qw, fr, wr, wp, rd, pg):
    pools = []
    for q in range(N):
        v = pl[q].reshape(128, 16 * PG, 4).copy()
        for s in range(N):
            c, p = entries(wr[s])[q * CW:q * CW + CW], entries(wp[q])[s * CW:s * CW + CW]
            k = p >= 0
            v[:, p[k]] = nw[s].reshape(128, NW, 4)[:, c[k]]
        pools.append(v)
    pools = np.concatenate(pools, axis=1)
    y = np.zeros((N, 128, O * SP * 16), np.float32)
    for r in range(N):
        e = (16 * entries(fr[r])[:, None] + np.arange(16)).reshape(-1)
        pages = mx_ref.quantize(np.ascontiguousarray(pools[:, e]).reshape(128, -1))
        for o in range(O):
            y[r][:, SP * 16 * o:SP * 16 * o + SP * 16] = mx_ref.matmul(mx_ref.quantize(np.ascontiguousarray(cut(qw[r], o))), pages)
    return {"y": y}

@@ -1,0 +1,259 @@
+from concourse.bass import DstId, RemoteDMATransfer
+from concourse.mybir import dt, AluOpType, ActivationFunctionType
+
+N = 8
+PG, NW, SP, CW, CP, O = 32, 64, 32, 16, 6, 2
+POOL = 16 * PG
+WIN = POOL + N * CW
+PC = 16 * CP
+ROW = POOL + 32
+DUMP = ROW + 1
+SROW = 800
+CH = 2
+CC = 16 * SP // CH
+
+F8, U8, U16, I32, F32, BF = "float8_e4m3fn_x4", "uint8", "uint16", "int32", "float32", "bfloat16"
+
+
+def _sb(n, d):
+    return ("sbuf", [128, n], d)
+
+
+SCRATCH = {
+    "nwt": _sb(512, BF), "plt": _sb(4 * POOL, BF), "qwt": _sb(512 * O, BF),
+    "lwr": _sb(8, I32), "lwp": _sb(8, I32), "lrd": _sb(4, I32), "lpg": _sb(2, I32),
+    "pcol": _sb(1, I32), "pand": _sb(2, I32), "cola": _sb(1, F32), "colb": _sb(1, F32), "colg": _sb(1, F32),
+    "ck": _sb(8, F32), "vals": _sb(128, F32), "cnt": _sb(ROW, F32), "cslot": _sb(48, F32), "wslot": _sb(48, F32),
+    "offa": _sb(8, U16), "offo": _sb(2, U16), "offw": _sb(8, U16), "offr": _sb(4, U16), "offb": _sb(48, U16),
+    "offg": _sb(2, U16), "offc": _sb(32, U16),
+    "w1": _sb(8, F32), "w2": _sb(8, F32), "w3": _sb(8, F32),
+    "r1": _sb(4, I32), "r2": _sb(4, I32), "r3": _sb(4, F32), "r4": _sb(4, F32), "r5": _sb(4, F32),
+    "srow": _sb(SROW, F32), "srct": _sb(ROW, F32),
+    "nwq": _sb(128, F8), "nws": _sb(128, U8),
+    "sndw": _sb(N * CW, F8), "sndws": _sb(N * CW, U8),
+    "win": _sb(WIN, F8), "wins": _sb(WIN, U8),
+    "sndp": _sb(N * PC, F8), "sndps": _sb(N * PC, U8),
+    "land": _sb(N * PC, F8), "lands": _sb(N * PC, U8),
+    "fin": _sb(16 * SP, F8), "fins": _sb(16 * SP, U8),
+    "qwq": _sb(128 * O, F8), "qws": _sb(128 * O, U8),
+    "ps": ("psum", [128, 512 * CH * O], F32),
+    "yb": _sb(512 * O, F32),
+}
+SEMAPHORES = (["dnw", "dwr", "dwp", "drd", "dpg", "dpl", "dqw", "ystore"]
+              + ["i_p", "i_k", "i_v", "i_c", "i_s"]
+              + ["v%d" % k for k in range(24)]
+              + ["nq", "oa", "oo", "oc", "ob", "plq", "qwd",
+                 "pka", "pkas", "owna", "ownas",
+                 "ownb", "ownbs"]
+              + ["pkb%d" % k for k in range(4)] + ["pkbs%d" % k for k in range(4)]
+              + ["fc%d" % k for k in range(CH)] + ["fs%d" % k for k in range(CH)]
+              + ["mm%d" % k for k in range(CH * O)] + ["cp%d" % k for k in range(CH * O)]
+              + ["arwc", "arws", "arpc", "arps", "left"])
+
+
+def _chips(T, topo):
+    chips = {}
+    for r, c in enumerate(T.cores):
+        chips.setdefault(topo.chip(c), []).append(r)
+    return [chips[k] for k in sorted(chips)]
+
+
+def _roads(T, topo, r):
+    chips = _chips(T, topo)
+    at = [k for k, m in enumerate(chips) if r in m][0]
+    away = [chips[(at + k) % len(chips)] for k in range(1, len(chips))]
+    near = [q for q in chips[at] if q != r]
+    out = topo.engines(T.cores[r], T.cores[away[0][0]])
+    inn = [e for e in topo.engines(T.cores[r], T.cores[near[0]]) if e not in out]
+    return away, near, out, inn
+
+
+def _deal(dests, engines):
+    k = len(engines) // len(dests)
+    return [(d, engines[k * i:k * i + k]) for i, d in enumerate(dests)]
+
+
+def _plan(T, topo, r, phase):
+    away, near, out, inn = _roads(T, topo, r)
+    if phase == "A":
+        return [_deal(away[0] + away[1], out) + _deal(near, inn[:2]), _deal(away[2], out)]
+    return [_deal(away[0], out), _deal(away[1] + away[2], out) + _deal(near, inn[:2])]
+
+
+def rank_program(g, core, T, topo):
+    me = T.rank_of(core)
+    if me is None:
+        return
+    S = T.sem
+    V, A, P, Y = g.vector, g.scalar, g.tensor, g.sync
+    Op, Copy = AluOpType, ActivationFunctionType.Copy
+    nv = [0]
+
+    def wait(q, *evs):
+        for e in evs:
+            n, k = e if isinstance(e, tuple) else (e, 1)
+            q.wait_ge(S[n], k)
+
+    def step(call):
+        n = "v%d" % nv[0]
+        nv[0] += 1
+        call.then_inc(S[n], 1)
+        return n
+
+    arrive = {}
+    for ph in "AB":
+        arrive[ph] = sum(len(e) for r in range(N) if r != me for call in _plan(T, topo, r, ph) for d, e in call if d == me)
+
+    def table(q, dst, src, cols, sem, groups):
+        for k in groups:
+            q.dma_start(dst[16 * k:16 * k + 16, 0:cols], src[:, :]).then_inc(S[sem], 16)
+
+    table(A, T.lwr, T.wr, 8, "dwr", range(0, 4))
+    Y.dma_start(T.nwt[:, 0:4 * NW], T.nw[:, :]).then_inc(S.dnw, 16)
+    table(Y, T.lwr, T.wr, 8, "dwr", range(4, 8))
+    table(Y, T.lwp, T.wp, 8, "dwp", range(8))
+    Y.dma_start(T.plt[:, :], T.pl[:, :]).then_inc(S.dpl, 16)
+
+    g.iota(T.pcol[:, :], [[1, 1]], 0, 1).then_inc(S.i_p, 1)
+    g.iota(T.ck[:, :], [[16, 8]], DUMP, 1, allow_small_or_imprecise_dtypes=True).then_inc(S.i_k, 1)
+    g.iota(T.vals[:, :], [[1, 128]], POOL, 0, allow_small_or_imprecise_dtypes=True).then_inc(S.i_v, 1)
+    g.iota(T.cslot[:, :], [[16, 48]], 0, 1, allow_small_or_imprecise_dtypes=True).then_inc(S.i_s, 1)
+    g.iota(T.cnt[:, :], [[1, ROW]], 0, 0, allow_small_or_imprecise_dtypes=True).then_inc(S.i_c, 1)
+
+    z = step(V.memset(T.nwt[:, 4 * NW:512], 0.0))
+    wait(V, "i_p")
+    a1 = step(V.tensor_scalar(T.pand[:, 0:1], T.pcol[:, 0:1], 16, None, Op.bitwise_and))
+    a2 = step(V.tensor_scalar(T.pand[:, 1:2], T.pcol[:, 0:1], 112, None, Op.bitwise_and))
+    wait(V, a1, a2)
+    a3 = step(V.tensor_copy(T.cola[:, :], T.pand[:, 0:1]))
+    a4 = step(V.tensor_copy(T.colg[:, :], T.pand[:, 1:2]))
+
+    wait(V, ("dwr", 128))
+    V.tensor_copy(T.offa[:, :], T.lwr[:, :]).then_inc(S.oa, 1)
+    wait(V, z, ("dnw", 16))
+    V.quantize_mx(T.nwq[:, :], T.nws[:, :], T.nwt[:, :]).then_inc(S.nq, 1)
+    wait(V, "oa", "nq")
+    V.tensor_copy(T.sndw[:, :].bitcast(dt.uint32), T.nwq[:, 0:NW].bitcast(dt.uint32).indirect(T.offa[:, 0:8])).then_inc(S.pka, 1)
+    V.tensor_copy(T.offo[:, 0:1], T.lwr[:, me:me + 1]).then_inc(S.oo, 1)
+    wait(V, "oo")
+    own = POOL + CW * me
+    V.tensor_copy(T.win[:, own:own + CW].bitcast(dt.uint32), T.nwq[:, 0:NW].bitcast(dt.uint32).indirect(T.offo[:, 0:1])).then_inc(S.owna, 1)
+
+    wait(A, "oa", "nq")
+    A.activation(T.sndws[:, :], T.nws[:, 0:NW].indirect(T.offa[:, 0:8]), Copy).then_inc(S.pkas, 1)
+    wait(A, "oo")
+    A.activation(T.wins[:, own:own + CW], T.nws[:, 0:NW].indirect(T.offo[:, 0:1]), Copy).then_inc(S.ownas, 1)
+    table(A, T.lrd, T.rd, 3, "drd", range(8))
+    A.dma_start(T.qwt[:, :], T.qw[:, :]).then_inc(S.dqw, 16)
+    table(A, T.lpg, T.pg, 2, "dpg", range(8))
+
+    left = [0]
+
+    def send(call, src, dst, w, to, codes, sem):
+        ts = []
+        for d, engines in call:
+            c = T.cores[d]
+            rid, pid, _ = topo.addr(c)
+            a, b = src[:, w * d:w * d + w], dst[:, to:to + w]
+            if codes:
+                a, b = a.bitcast(dt.uint8), b.bitcast(dt.uint8)
+            left[0] += len(engines)
+            ts.append(RemoteDMATransfer(dst_ids=[DstId(rid=rid, pnc=pid)], dma_engine_mask=sum(1 << e for e in engines),
+                                        remote_sem=S[sem], src=a, dst=b))
+        g.remote_dma_fused(ts, local_sem=S.left)
+
+    plan = _plan(T, topo, me, "A")
+    for k, call in enumerate(plan):
+        if k == 0:
+            wait(g, "pka")
+        send(call, T.sndw, T.win, CW, own, True, "arwc")
+        if k == 0:
+            wait(g, "pkas")
+        send(call, T.sndws, T.wins, CW, own, False, "arws")
+
+    wait(V, "i_c", a3, a4, ("dwp", 128), "i_k")
+    b1 = step(V.tensor_scalar(T.w1[:, :], T.lwp[:, :], 0, None, Op.is_lt))
+    b0 = step(V.tensor_scalar(T.srow[:, 0:ROW], T.cnt[:, :], T.cola[:, 0:1], None, Op.subtract))
+    wait(V, b1)
+    b2 = step(V.tensor_tensor(T.w2[:, :], T.w1[:, :], T.ck[:, :], Op.mult))
+    wait(V, b2)
+    b3 = step(V.tensor_tensor(T.w3[:, :], T.w2[:, :], T.lwp[:, :], Op.add))
+    wait(V, b3)
+    b4 = step(V.tensor_scalar(T.offw[:, :], T.w3[:, :], T.cola[:, 0:1], None, Op.add))
+    wait(V, b0, b4, "i_v")
+    b5 = step(V.tensor_copy(T.srow[:, :].indirect(T.offw[:, :]), T.vals[:, :]))
+    b6 = step(V.tensor_scalar(T.colb[:, :], T.cola[:, :], -4.0, 32.0, Op.mult, Op.add))
+    wait(V, ("drd", 128))
+    c1 = step(V.tensor_scalar(T.r1[:, 0:3], T.lrd[:, 0:3], 0, None, Op.max))
+    wait(V, c1)
+    c2 = step(V.tensor_scalar(T.r2[:, 0:3], T.r1[:, 0:3], 1, None, Op.bitwise_and))
+    c3 = step(V.tensor_scalar(T.r3[:, 0:3], T.r1[:, 0:3], 16.0, None, Op.mult))
+    wait(V, c2, b6)
+    c4 = step(V.tensor_scalar(T.r4[:, 0:3], T.r2[:, 0:3], T.colb[:, 0:1], T.cola[:, 0:1], Op.mult, Op.add))
+    wait(V, c3, c4)
+    c5 = step(V.tensor_tensor(T.r5[:, 0:3], T.r3[:, 0:3], T.r4[:, 0:3], Op.add))
+    wait(V, b5)
+    b7 = step(V.transpose(T.srct[:, :], T.srow[:, 0:ROW]))
+    wait(V, c5)
+    c6 = step(V.tensor_copy(T.offr[:, 0:3], T.r5[:, 0:3]))
+    wait(V, b7, c6)
+    V.tensor_copy(T.offb[:, :], T.srct[:, :].indirect(T.offr[:, 0:3])).then_inc(S.ob, 1)
+    wait(V, ("dpl", 16))
+    V.quantize_mx(T.win[:, 0:POOL], T.wins[:, 0:POOL], T.plt[:, :]).then_inc(S.plq, 1)
+    wait(V, "i_s")
+    e1 = step(V.tensor_scalar(T.wslot[:, :], T.cslot[:, :], T.colg[:, 0:1], None, Op.subtract))
+    wait(V, ("dqw", 16))
+    V.quantize_mx(T.qwq[:, :], T.qws[:, :], T.qwt[:, :]).then_inc(S.qwd, 1)
+    wait(V, ("dpg", 128))
+    e2 = step(V.tensor_copy(T.offg[:, :], T.lpg[:, :]))
+    wait(V, e1, e2)
+    V.tensor_copy(T.offc[:, :], T.wslot[:, :].indirect(T.offg[:, 0:2])).then_inc(S.oc, 1)
+
+    away, near, _, _ = _roads(T, topo, me)
+    picks = [(m[0], len(m), "sndp", "pkb%d" % k) for k, m in enumerate(away)]
+    picks += [(near[0], 1, "sndp", "pkb3"), (me, 1, "land", "ownb")]
+    wait(V, "owna", "plq", "ob", ("arwc", arrive["A"]))
+    for r, n, buf, ev in picks:
+        V.tensor_copy(T[buf][:, PC * r:PC * (r + n)].bitcast(dt.uint32),
+                      T.win[:, :].bitcast(dt.uint32).indirect(T.offb[:, CP * r:CP * (r + n)])).then_inc(S[ev], 1)
+    wait(A, "ownas", "plq", "ob", ("arws", arrive["A"]))
+    for r, n, buf, ev in picks:
+        A.activation(T[buf + "s"][:, PC * r:PC * (r + n)], T.wins[:, :].indirect(T.offb[:, CP * r:CP * (r + n)]),
+                     Copy).then_inc(S[ev.replace("pkb", "pkbs").replace("ownb", "ownbs")], 1)
+    plan = _plan(T, topo, me, "B")
+    for k, call in enumerate(plan):
+        need = (0,) if k == 0 else (1, 2, 3)
+        wait(g, *["pkb%d" % i for i in need])
+        send(call, T.sndp, T.land, PC, PC * me, True, "arpc")
+        wait(g, *["pkbs%d" % i for i in need])
+        send(call, T.sndps, T.lands, PC, PC * me, False, "arps")
+    g.wait_ge(S.left, left[0])
+
+    wait(V, "ownb", "oc", ("arpc", arrive["B"]))
+    wait(A, "ownbs", "oc", ("arps", arrive["B"]))
+    for c in range(CH):
+        lo, k = CC * c, CC // 16
+        V.tensor_copy(T.fin[:, lo:lo + CC].bitcast(dt.uint32),
+                      T.land[:, :].bitcast(dt.uint32).indirect(T.offc[:, k * c:k * c + k])).then_inc(S["fc%d" % c], 1)
+        A.activation(T.fins[:, lo:lo + CC], T.lands[:, :].indirect(T.offc[:, k * c:k * c + k]), Copy).then_inc(S["fs%d" % c], 1)
+    wait(P, "qwd")
+    for c in range(CH):
+        lo = CC * c
+        wait(P, "fc%d" % c, "fs%d" % c)
+        for o in range(O):
+            b = O * c + o
+            P.matmul_mx(T.ps[:, 512 * b:512 * b + CC], T.qwq[:, 128 * o:128 * o + 128], T.qws[:, 128 * o:128 * o + 128],
+                        T.fin[:, lo:lo + CC], T.fins[:, lo:lo + CC], True, True).then_inc(S["mm%d" % b], 1)
+    for c in range(CH):
+        for o in range(O):
+            b, at = O * c + o, 512 * o + CC * c
+            q = V if o == 0 else A
+            wait(q, "mm%d" % b)
+            if o == 0:
+                V.tensor_copy(T.yb[:, at:at + CC], T.ps[:, 512 * b:512 * b + CC]).then_inc(S["cp%d" % b], 1)
+            else:
+                A.activation(T.yb[:, at:at + CC], T.ps[:, 512 * b:512 * b + CC], Copy).then_inc(S["cp%d" % b], 1)
+            d = A if b == CH * O - 1 else Y
+            wait(d, "cp%d" % b)
+            d.dma_start(T.y[:, at:at + CC], T.yb[:, at:at + CC]).then_inc(S.ystore, 16)
+    Y.wait_ge(S.ystore, 16 * CH * O)

@@ -7,9 +7,9 @@ POOL = 16 * PG
 WIN = POOL + N * CW
 PC = 16 * CP
 ROW = POOL + 32
-DUMP = ROW + 1
+DUMP = ROW - 16
 SROW = 800
-CH = 2
+CH = 4
 CC = 16 * SP // CH
 
 F8, U8, U16, I32, F32, BF = "float8_e4m3fn_x4", "uint8", "uint16", "int32", "float32", "bfloat16"
@@ -22,12 +22,11 @@ def _sb(n, d):
 SCRATCH = {
     "nwt": _sb(512, BF), "plt": _sb(4 * POOL, BF), "qwt": _sb(512 * O, BF),
     "lwr": _sb(8, I32), "lwp": _sb(8, I32), "lrd": _sb(4, I32), "lpg": _sb(2, I32),
-    "pcol": _sb(1, I32), "pand": _sb(2, I32), "cola": _sb(1, F32), "colb": _sb(1, F32), "colg": _sb(1, F32),
-    "ck": _sb(8, F32), "vals": _sb(128, F32), "cnt": _sb(ROW, F32), "cslot": _sb(48, F32), "wslot": _sb(48, F32),
+    "pcol": _sb(1, I32), "pand": _sb(2, I32), "cold": _sb(1, F32), "coln": _sb(1, F32), "colg": _sb(1, F32),
+    "ck": _sb(8, I32), "cnt": _sb(WIN, F32), "cslot": _sb(48, F32), "wslot": _sb(48, F32),
     "offa": _sb(8, U16), "offo": _sb(2, U16), "offw": _sb(8, U16), "offr": _sb(4, U16), "offb": _sb(48, U16),
     "offg": _sb(2, U16), "offc": _sb(32, U16),
-    "w1": _sb(8, F32), "w2": _sb(8, F32), "w3": _sb(8, F32),
-    "r1": _sb(4, I32), "r2": _sb(4, I32), "r3": _sb(4, F32), "r4": _sb(4, F32), "r5": _sb(4, F32),
+    "w1": _sb(8, I32), "w2": _sb(8, F32), "r1": _sb(4, F32),
     "srow": _sb(SROW, F32), "srct": _sb(ROW, F32),
     "nwq": _sb(128, F8), "nws": _sb(128, U8),
     "sndw": _sb(N * CW, F8), "sndws": _sb(N * CW, U8),
@@ -40,7 +39,7 @@ SCRATCH = {
     "yb": _sb(512 * O, F32),
 }
 SEMAPHORES = (["dnw", "dwr", "dwp", "drd", "dpg", "dpl", "dqw", "ystore"]
-              + ["i_p", "i_k", "i_v", "i_c", "i_s"]
+              + ["i_p", "i_k", "i_c", "i_s", "cn", "row"]
               + ["v%d" % k for k in range(24)]
               + ["nq", "oa", "oo", "oc", "ob", "plq", "qwd",
                  "pka", "pkas", "owna", "ownas",
@@ -109,24 +108,24 @@ def rank_program(g, core, T, topo):
             q.dma_start(dst[16 * k:16 * k + 16, 0:cols], src[:, :]).then_inc(S[sem], 16)
 
     table(A, T.lwr, T.wr, 8, "dwr", range(0, 4))
+    A.dma_start(T.qwt[:, :], T.qw[:, :]).then_inc(S.dqw, 16)
     Y.dma_start(T.nwt[:, 0:4 * NW], T.nw[:, :]).then_inc(S.dnw, 16)
     table(Y, T.lwr, T.wr, 8, "dwr", range(4, 8))
-    table(Y, T.lwp, T.wp, 8, "dwp", range(8))
     Y.dma_start(T.plt[:, :], T.pl[:, :]).then_inc(S.dpl, 16)
+    table(Y, T.lwp, T.wp, 8, "dwp", range(8))
+    table(Y, T.lrd, T.rd, 3, "drd", range(8))
+    table(Y, T.lpg, T.pg, 2, "dpg", range(8))
 
     g.iota(T.pcol[:, :], [[1, 1]], 0, 1).then_inc(S.i_p, 1)
-    g.iota(T.ck[:, :], [[16, 8]], DUMP, 1, allow_small_or_imprecise_dtypes=True).then_inc(S.i_k, 1)
-    g.iota(T.vals[:, :], [[1, 128]], POOL, 0, allow_small_or_imprecise_dtypes=True).then_inc(S.i_v, 1)
-    g.iota(T.cslot[:, :], [[16, 48]], 0, 1, allow_small_or_imprecise_dtypes=True).then_inc(S.i_s, 1)
-    g.iota(T.cnt[:, :], [[1, ROW]], 0, 0, allow_small_or_imprecise_dtypes=True).then_inc(S.i_c, 1)
+    g.iota(T.ck[:, :], [[16, 8]], DUMP, 1).then_inc(S.i_k, 1)
+    g.iota(T.cnt[:, :], [[1, WIN]], 0, 0, allow_small_or_imprecise_dtypes=True).then_inc(S.i_c, 1)
 
     z = step(V.memset(T.nwt[:, 4 * NW:512], 0.0))
     wait(V, "i_p")
     a1 = step(V.tensor_scalar(T.pand[:, 0:1], T.pcol[:, 0:1], 16, None, Op.bitwise_and))
-    a2 = step(V.tensor_scalar(T.pand[:, 1:2], T.pcol[:, 0:1], 112, None, Op.bitwise_and))
-    wait(V, a1, a2)
-    a3 = step(V.tensor_copy(T.cola[:, :], T.pand[:, 0:1]))
-    a4 = step(V.tensor_copy(T.colg[:, :], T.pand[:, 1:2]))
+    wait(V, a1)
+    V.tensor_scalar(T.coln[:, :], T.pand[:, 0:1], 32.0, None, Op.subtract).then_inc(S.cn, 1)
+    a2 = step(V.tensor_scalar(T.cold[:, :], T.pand[:, 0:1], -1.0, 32.0, Op.mult, Op.add))
 
     wait(V, ("dwr", 128))
     V.tensor_copy(T.offa[:, :], T.lwr[:, :]).then_inc(S.oa, 1)
@@ -135,17 +134,14 @@ def rank_program(g, core, T, topo):
     wait(V, "oa", "nq")
     V.tensor_copy(T.sndw[:, :].bitcast(dt.uint32), T.nwq[:, 0:NW].bitcast(dt.uint32).indirect(T.offa[:, 0:8])).then_inc(S.pka, 1)
     V.tensor_copy(T.offo[:, 0:1], T.lwr[:, me:me + 1]).then_inc(S.oo, 1)
-    wait(V, "oo")
     own = POOL + CW * me
-    V.tensor_copy(T.win[:, own:own + CW].bitcast(dt.uint32), T.nwq[:, 0:NW].bitcast(dt.uint32).indirect(T.offo[:, 0:1])).then_inc(S.owna, 1)
 
     wait(A, "oa", "nq")
     A.activation(T.sndws[:, :], T.nws[:, 0:NW].indirect(T.offa[:, 0:8]), Copy).then_inc(S.pkas, 1)
+    wait(A, "i_c", "cn")
+    A.activation(T.srow[:, 0:ROW], T.cnt[:, 0:ROW], ActivationFunctionType.Identity, bias=T.coln[:, 0:1]).then_inc(S.row, 1)
     wait(A, "oo")
     A.activation(T.wins[:, own:own + CW], T.nws[:, 0:NW].indirect(T.offo[:, 0:1]), Copy).then_inc(S.ownas, 1)
-    table(A, T.lrd, T.rd, 3, "drd", range(8))
-    A.dma_start(T.qwt[:, :], T.qw[:, :]).then_inc(S.dqw, 16)
-    table(A, T.lpg, T.pg, 2, "dpg", range(8))
 
     left = [0]
 
@@ -163,51 +159,34 @@ def rank_program(g, core, T, topo):
         g.remote_dma_fused(ts, local_sem=S.left)
 
     plan = _plan(T, topo, me, "A")
-    for k, call in enumerate(plan):
-        if k == 0:
-            wait(g, "pka")
+    wait(g, "pka")
+    for call in plan:
         send(call, T.sndw, T.win, CW, own, True, "arwc")
-        if k == 0:
-            wait(g, "pkas")
+    wait(g, "pkas")
+    for call in plan:
         send(call, T.sndws, T.wins, CW, own, False, "arws")
+    g.iota(T.cslot[:, :], [[16, 48]], 0, 1, allow_small_or_imprecise_dtypes=True).then_inc(S.i_s, 1)
 
-    wait(V, "i_c", a3, a4, ("dwp", 128), "i_k")
-    b1 = step(V.tensor_scalar(T.w1[:, :], T.lwp[:, :], 0, None, Op.is_lt))
-    b0 = step(V.tensor_scalar(T.srow[:, 0:ROW], T.cnt[:, :], T.cola[:, 0:1], None, Op.subtract))
-    wait(V, b1)
-    b2 = step(V.tensor_tensor(T.w2[:, :], T.w1[:, :], T.ck[:, :], Op.mult))
-    wait(V, b2)
-    b3 = step(V.tensor_tensor(T.w3[:, :], T.w2[:, :], T.lwp[:, :], Op.add))
-    wait(V, b3)
-    b4 = step(V.tensor_scalar(T.offw[:, :], T.w3[:, :], T.cola[:, 0:1], None, Op.add))
-    wait(V, b0, b4, "i_v")
-    b5 = step(V.tensor_copy(T.srow[:, :].indirect(T.offw[:, :]), T.vals[:, :]))
-    b6 = step(V.tensor_scalar(T.colb[:, :], T.cola[:, :], -4.0, 32.0, Op.mult, Op.add))
+    wait(V, ("dwp", 128), "i_k", a2)
+    b1 = step(V.tensor_scalar(T.w1[:, :], T.lwp[:, :], 1023, None, Op.bitwise_and))
     wait(V, ("drd", 128))
-    c1 = step(V.tensor_scalar(T.r1[:, 0:3], T.lrd[:, 0:3], 0, None, Op.max))
+    c1 = step(V.tensor_scalar(T.r1[:, 0:3], T.lrd[:, 0:3], 0.0, 16.0, Op.max, Op.mult))
+    wait(V, b1)
+    b2 = step(V.tensor_tensor(T.w2[:, :], T.w1[:, :], T.ck[:, :], Op.min))
     wait(V, c1)
-    c2 = step(V.tensor_scalar(T.r2[:, 0:3], T.r1[:, 0:3], 1, None, Op.bitwise_and))
-    c3 = step(V.tensor_scalar(T.r3[:, 0:3], T.r1[:, 0:3], 16.0, None, Op.mult))
-    wait(V, c2, b6)
-    c4 = step(V.tensor_scalar(T.r4[:, 0:3], T.r2[:, 0:3], T.colb[:, 0:1], T.cola[:, 0:1], Op.mult, Op.add))
-    wait(V, c3, c4)
-    c5 = step(V.tensor_tensor(T.r5[:, 0:3], T.r3[:, 0:3], T.r4[:, 0:3], Op.add))
-    wait(V, b5)
-    b7 = step(V.transpose(T.srct[:, :], T.srow[:, 0:ROW]))
-    wait(V, c5)
-    c6 = step(V.tensor_copy(T.offr[:, 0:3], T.r5[:, 0:3]))
-    wait(V, b7, c6)
+    c2 = step(V.tensor_scalar(T.offr[:, 0:3], T.r1[:, 0:3], T.cold[:, 0:1], None, Op.add))
+    wait(V, b2)
+    b3 = step(V.tensor_scalar(T.offw[:, :], T.w2[:, :], T.cold[:, 0:1], None, Op.add))
+    wait(V, b3, "row", "i_c")
+    b4 = step(V.tensor_copy(T.srow[:, :].indirect(T.offw[:, :]), T.cnt[:, POOL:WIN]))
+    wait(V, b4)
+    b5 = step(V.transpose(T.srct[:, :], T.srow[:, 0:ROW]))
+    wait(V, "oo")
+    V.tensor_copy(T.win[:, own:own + CW].bitcast(dt.uint32), T.nwq[:, 0:NW].bitcast(dt.uint32).indirect(T.offo[:, 0:1])).then_inc(S.owna, 1)
+    wait(V, b5, c2)
     V.tensor_copy(T.offb[:, :], T.srct[:, :].indirect(T.offr[:, 0:3])).then_inc(S.ob, 1)
     wait(V, ("dpl", 16))
     V.quantize_mx(T.win[:, 0:POOL], T.wins[:, 0:POOL], T.plt[:, :]).then_inc(S.plq, 1)
-    wait(V, "i_s")
-    e1 = step(V.tensor_scalar(T.wslot[:, :], T.cslot[:, :], T.colg[:, 0:1], None, Op.subtract))
-    wait(V, ("dqw", 16))
-    V.quantize_mx(T.qwq[:, :], T.qws[:, :], T.qwt[:, :]).then_inc(S.qwd, 1)
-    wait(V, ("dpg", 128))
-    e2 = step(V.tensor_copy(T.offg[:, :], T.lpg[:, :]))
-    wait(V, e1, e2)
-    V.tensor_copy(T.offc[:, :], T.wslot[:, :].indirect(T.offg[:, 0:2])).then_inc(S.oc, 1)
 
     away, near, _, _ = _roads(T, topo, me)
     picks = [(m[0], len(m), "sndp", "pkb%d" % k) for k, m in enumerate(away)]
@@ -221,39 +200,55 @@ def rank_program(g, core, T, topo):
         A.activation(T[buf + "s"][:, PC * r:PC * (r + n)], T.wins[:, :].indirect(T.offb[:, CP * r:CP * (r + n)]),
                      Copy).then_inc(S[ev.replace("pkb", "pkbs").replace("ownb", "ownbs")], 1)
     plan = _plan(T, topo, me, "B")
+    need = ((0,), (1, 2, 3))
     for k, call in enumerate(plan):
-        need = (0,) if k == 0 else (1, 2, 3)
-        wait(g, *["pkb%d" % i for i in need])
+        wait(g, *["pkb%d" % i for i in need[k]])
         send(call, T.sndp, T.land, PC, PC * me, True, "arpc")
-        wait(g, *["pkbs%d" % i for i in need])
+    for k, call in enumerate(plan):
+        wait(g, *["pkbs%d" % i for i in need[k]])
         send(call, T.sndps, T.lands, PC, PC * me, False, "arps")
     g.wait_ge(S.left, left[0])
 
+    wait(V, ("dqw", 16))
+    V.quantize_mx(T.qwq[:, :], T.qws[:, :], T.qwt[:, :]).then_inc(S.qwd, 1)
+    wait(V, "i_p")
+    e1 = step(V.tensor_scalar(T.pand[:, 1:2], T.pcol[:, 0:1], 112, None, Op.bitwise_and))
+    wait(V, ("dpg", 128))
+    e2 = step(V.tensor_copy(T.offg[:, :], T.lpg[:, :]))
+    wait(V, e1)
+    e3 = step(V.tensor_copy(T.colg[:, :], T.pand[:, 1:2]))
+    wait(V, e3, "i_s")
+    e4 = step(V.tensor_scalar(T.wslot[:, :], T.cslot[:, :], T.colg[:, 0:1], None, Op.subtract))
+    wait(V, e2, e4)
+    V.tensor_copy(T.offc[:, :], T.wslot[:, :].indirect(T.offg[:, 0:2])).then_inc(S.oc, 1)
+
+    k = CC // 16
     wait(V, "ownb", "oc", ("arpc", arrive["B"]))
-    wait(A, "ownbs", "oc", ("arps", arrive["B"]))
     for c in range(CH):
-        lo, k = CC * c, CC // 16
-        V.tensor_copy(T.fin[:, lo:lo + CC].bitcast(dt.uint32),
+        V.tensor_copy(T.fin[:, CC * c:CC * c + CC].bitcast(dt.uint32),
                       T.land[:, :].bitcast(dt.uint32).indirect(T.offc[:, k * c:k * c + k])).then_inc(S["fc%d" % c], 1)
-        A.activation(T.fins[:, lo:lo + CC], T.lands[:, :].indirect(T.offc[:, k * c:k * c + k]), Copy).then_inc(S["fs%d" % c], 1)
-    wait(P, "qwd")
+    for q in (V, A):
+        wait(q, "ownbs", "oc", ("arps", arrive["B"]))
     for c in range(CH):
-        lo = CC * c
-        wait(P, "fc%d" % c, "fs%d" % c)
-        for o in range(O):
+        a, b = T.fins[:, CC * c:CC * c + CC], T.lands[:, :].indirect(T.offc[:, k * c:k * c + k])
+        (A.activation(a, b, Copy) if c % 2 else V.tensor_copy(a, b)).then_inc(S["fs%d" % c], 1)
+    wait(P, "qwd")
+    half = [(h, o) for h in range(2) for o in range(O)]
+    for h, o in half:
+        for c in (2 * h, 2 * h + 1):
+            if o == 0:
+                wait(P, "fc%d" % c, "fs%d" % c)
             b = O * c + o
             P.matmul_mx(T.ps[:, 512 * b:512 * b + CC], T.qwq[:, 128 * o:128 * o + 128], T.qws[:, 128 * o:128 * o + 128],
-                        T.fin[:, lo:lo + CC], T.fins[:, lo:lo + CC], True, True).then_inc(S["mm%d" % b], 1)
-    for c in range(CH):
-        for o in range(O):
+                        T.fin[:, CC * c:CC * c + CC], T.fins[:, CC * c:CC * c + CC], True, True).then_inc(S["mm%d" % b], 1)
+    for h, o in half:
+        for c in (2 * h, 2 * h + 1):
             b, at = O * c + o, 512 * o + CC * c
-            q = V if o == 0 else A
+            q = A if c % 2 else V
             wait(q, "mm%d" % b)
-            if o == 0:
-                V.tensor_copy(T.yb[:, at:at + CC], T.ps[:, 512 * b:512 * b + CC]).then_inc(S["cp%d" % b], 1)
-            else:
-                A.activation(T.yb[:, at:at + CC], T.ps[:, 512 * b:512 * b + CC], Copy).then_inc(S["cp%d" % b], 1)
-            d = A if b == CH * O - 1 else Y
-            wait(d, "cp%d" % b)
-            d.dma_start(T.y[:, at:at + CC], T.yb[:, at:at + CC]).then_inc(S.ystore, 16)
-    Y.wait_ge(S.ystore, 16 * CH * O)
+            u, v = T.yb[:, at:at + CC], T.ps[:, 512 * b:512 * b + CC]
+            (A.activation(u, v, Copy) if c % 2 else V.tensor_copy(u, v)).then_inc(S["cp%d" % b], 1)
+            wait(Y, "cp%d" % b)
+        at = 512 * o + 2 * CC * h
+        Y.dma_start(T.y[:, at:at + 2 * CC], T.yb[:, at:at + 2 * CC]).then_inc(S.ystore, 16)
+    Y.wait_ge(S.ystore, 16 * len(half))

from concourse.bass import DstId, RemoteDMATransfer
from concourse.mybir import dt, AluOpType, ActivationFunctionType

N = 8
PG, NW, SP, CW, CP, O = 32, 64, 32, 16, 6, 2
POOL = 16 * PG
WIN = POOL + N * CW
PC = 16 * CP
ROW = POOL + 32
DUMP = ROW - 16
SROW = 800
CH = 4
CC = 16 * SP // CH

F8, U8, U16, I32, F32, BF = "float8_e4m3fn_x4", "uint8", "uint16", "int32", "float32", "bfloat16"


def _sb(n, d):
    return ("sbuf", [128, n], d)


SCRATCH = {
    "nwt": _sb(512, BF), "plt": _sb(4 * POOL, BF), "qwt": _sb(512 * O, BF),
    "lwr": _sb(8, I32), "lwp": _sb(8, I32), "lrd": _sb(4, I32), "lpg": _sb(2, I32),
    "pcol": _sb(1, I32), "pand": _sb(2, I32), "cold": _sb(1, F32), "coln": _sb(1, F32), "colg": _sb(1, F32),
    "ck": _sb(8, I32), "cnt": _sb(WIN, F32), "cslot": _sb(48, F32), "wslot": _sb(48, F32),
    "offa": _sb(8, U16), "offo": _sb(2, U16), "offw": _sb(8, U16), "offr": _sb(4, U16), "offb": _sb(48, U16),
    "offg": _sb(2, U16), "offc": _sb(32, U16),
    "w1": _sb(8, I32), "w2": _sb(8, F32), "r1": _sb(4, F32),
    "srow": _sb(SROW, F32), "srct": _sb(ROW, F32),
    "nwq": _sb(128, F8), "nws": _sb(128, U8),
    "sndw": _sb(N * CW, F8), "sndws": _sb(N * CW, U8),
    "win": _sb(WIN, F8), "wins": _sb(WIN, U8),
    "sndp": _sb(N * PC, F8), "sndps": _sb(N * PC, U8),
    "land": _sb(N * PC, F8), "lands": _sb(N * PC, U8),
    "fin": _sb(16 * SP, F8), "fins": _sb(16 * SP, U8),
    "qwq": _sb(128 * O, F8), "qws": _sb(128 * O, U8),
    "ps": ("psum", [128, 512 * CH * O], F32),
    "yb": _sb(512 * O, F32),
}
SEMAPHORES = (["dnw", "dwr", "dwp", "drd", "dpg", "dpl", "dqw", "ystore"]
              + ["i_p", "i_k", "i_c", "i_s", "cn", "row"]
              + ["v%d" % k for k in range(24)]
              + ["nq", "oa", "oo", "oc", "ob", "plq", "qwd",
                 "pka", "pkas", "owna", "ownas",
                 "ownb", "ownbs"]
              + ["pkb%d" % k for k in range(4)] + ["pkbs%d" % k for k in range(4)]
              + ["fc%d" % k for k in range(CH)] + ["fs%d" % k for k in range(CH)]
              + ["mm%d" % k for k in range(CH * O)] + ["cp%d" % k for k in range(CH * O)]
              + ["arwc", "arws", "arpc", "arps", "left"])


def _chips(T, topo):
    chips = {}
    for r, c in enumerate(T.cores):
        chips.setdefault(topo.chip(c), []).append(r)
    return [chips[k] for k in sorted(chips)]


def _roads(T, topo, r):
    chips = _chips(T, topo)
    at = [k for k, m in enumerate(chips) if r in m][0]
    away = [chips[(at + k) % len(chips)] for k in range(1, len(chips))]
    near = [q for q in chips[at] if q != r]
    out = topo.engines(T.cores[r], T.cores[away[0][0]])
    inn = [e for e in topo.engines(T.cores[r], T.cores[near[0]]) if e not in out]
    return away, near, out, inn


def _deal(dests, engines):
    k = len(engines) // len(dests)
    return [(d, engines[k * i:k * i + k]) for i, d in enumerate(dests)]


def _plan(T, topo, r, phase):
    away, near, out, inn = _roads(T, topo, r)
    if phase == "A":
        return [_deal(away[0] + away[1], out) + _deal(near, inn[:2]), _deal(away[2], out)]
    return [_deal(away[0], out), _deal(away[1] + away[2], out) + _deal(near, inn[:2])]


def rank_program(g, core, T, topo):
    me = T.rank_of(core)
    if me is None:
        return
    S = T.sem
    V, A, P, Y = g.vector, g.scalar, g.tensor, g.sync
    Op, Copy = AluOpType, ActivationFunctionType.Copy
    nv = [0]

    def wait(q, *evs):
        for e in evs:
            n, k = e if isinstance(e, tuple) else (e, 1)
            q.wait_ge(S[n], k)

    def step(call):
        n = "v%d" % nv[0]
        nv[0] += 1
        call.then_inc(S[n], 1)
        return n

    arrive = {}
    for ph in "AB":
        arrive[ph] = sum(len(e) for r in range(N) if r != me for call in _plan(T, topo, r, ph) for d, e in call if d == me)

    def table(q, dst, src, cols, sem, groups):
        for k in groups:
            q.dma_start(dst[16 * k:16 * k + 16, 0:cols], src[:, :]).then_inc(S[sem], 16)

    table(A, T.lwr, T.wr, 8, "dwr", range(0, 4))
    A.dma_start(T.qwt[:, :], T.qw[:, :]).then_inc(S.dqw, 16)
    Y.dma_start(T.nwt[:, 0:4 * NW], T.nw[:, :]).then_inc(S.dnw, 16)
    table(Y, T.lwr, T.wr, 8, "dwr", range(4, 8))
    Y.dma_start(T.plt[:, :], T.pl[:, :]).then_inc(S.dpl, 16)
    table(Y, T.lwp, T.wp, 8, "dwp", range(8))
    table(Y, T.lrd, T.rd, 3, "drd", range(8))
    table(Y, T.lpg, T.pg, 2, "dpg", range(8))

    g.iota(T.pcol[:, :], [[1, 1]], 0, 1).then_inc(S.i_p, 1)
    g.iota(T.ck[:, :], [[16, 8]], DUMP, 1).then_inc(S.i_k, 1)
    g.iota(T.cnt[:, :], [[1, WIN]], 0, 0, allow_small_or_imprecise_dtypes=True).then_inc(S.i_c, 1)

    z = step(V.memset(T.nwt[:, 4 * NW:512], 0.0))
    wait(V, "i_p")
    a1 = step(V.tensor_scalar(T.pand[:, 0:1], T.pcol[:, 0:1], 16, None, Op.bitwise_and))
    wait(V, a1)
    V.tensor_scalar(T.coln[:, :], T.pand[:, 0:1], 32.0, None, Op.subtract).then_inc(S.cn, 1)
    a2 = step(V.tensor_scalar(T.cold[:, :], T.pand[:, 0:1], -1.0, 32.0, Op.mult, Op.add))

    wait(V, ("dwr", 128))
    V.tensor_copy(T.offa[:, :], T.lwr[:, :]).then_inc(S.oa, 1)
    wait(V, z, ("dnw", 16))
    V.quantize_mx(T.nwq[:, :], T.nws[:, :], T.nwt[:, :]).then_inc(S.nq, 1)
    wait(V, "oa", "nq")
    V.tensor_copy(T.sndw[:, :].bitcast(dt.uint32), T.nwq[:, 0:NW].bitcast(dt.uint32).indirect(T.offa[:, 0:8])).then_inc(S.pka, 1)
    V.tensor_copy(T.offo[:, 0:1], T.lwr[:, me:me + 1]).then_inc(S.oo, 1)
    own = POOL + CW * me

    wait(A, "oa", "nq")
    A.activation(T.sndws[:, :], T.nws[:, 0:NW].indirect(T.offa[:, 0:8]), Copy).then_inc(S.pkas, 1)
    wait(A, "i_c", "cn")
    A.activation(T.srow[:, 0:ROW], T.cnt[:, 0:ROW], ActivationFunctionType.Identity, bias=T.coln[:, 0:1]).then_inc(S.row, 1)
    wait(A, "oo")
    A.activation(T.wins[:, own:own + CW], T.nws[:, 0:NW].indirect(T.offo[:, 0:1]), Copy).then_inc(S.ownas, 1)

    left = [0]

    def send(call, src, dst, w, to, codes, sem):
        ts = []
        for d, engines in call:
            c = T.cores[d]
            rid, pid, _ = topo.addr(c)
            a, b = src[:, w * d:w * d + w], dst[:, to:to + w]
            if codes:
                a, b = a.bitcast(dt.uint8), b.bitcast(dt.uint8)
            left[0] += len(engines)
            ts.append(RemoteDMATransfer(dst_ids=[DstId(rid=rid, pnc=pid)], dma_engine_mask=sum(1 << e for e in engines),
                                        remote_sem=S[sem], src=a, dst=b))
        g.remote_dma_fused(ts, local_sem=S.left)

    plan = _plan(T, topo, me, "A")
    wait(g, "pka")
    for call in plan:
        send(call, T.sndw, T.win, CW, own, True, "arwc")
    wait(g, "pkas")
    for call in plan:
        send(call, T.sndws, T.wins, CW, own, False, "arws")
    g.iota(T.cslot[:, :], [[16, 48]], 0, 1, allow_small_or_imprecise_dtypes=True).then_inc(S.i_s, 1)

    wait(V, ("dwp", 128), "i_k", a2)
    b1 = step(V.tensor_scalar(T.w1[:, :], T.lwp[:, :], 1023, None, Op.bitwise_and))
    wait(V, ("drd", 128))
    c1 = step(V.tensor_scalar(T.r1[:, 0:3], T.lrd[:, 0:3], 0.0, 16.0, Op.max, Op.mult))
    wait(V, b1)
    b2 = step(V.tensor_tensor(T.w2[:, :], T.w1[:, :], T.ck[:, :], Op.min))
    wait(V, c1)
    c2 = step(V.tensor_scalar(T.offr[:, 0:3], T.r1[:, 0:3], T.cold[:, 0:1], None, Op.add))
    wait(V, b2)
    b3 = step(V.tensor_scalar(T.offw[:, :], T.w2[:, :], T.cold[:, 0:1], None, Op.add))
    wait(V, b3, "row", "i_c")
    b4 = step(V.tensor_copy(T.srow[:, :].indirect(T.offw[:, :]), T.cnt[:, POOL:WIN]))
    wait(V, b4)
    b5 = step(V.transpose(T.srct[:, :], T.srow[:, 0:ROW]))
    wait(V, "oo")
    V.tensor_copy(T.win[:, own:own + CW].bitcast(dt.uint32), T.nwq[:, 0:NW].bitcast(dt.uint32).indirect(T.offo[:, 0:1])).then_inc(S.owna, 1)
    wait(V, b5, c2)
    V.tensor_copy(T.offb[:, :], T.srct[:, :].indirect(T.offr[:, 0:3])).then_inc(S.ob, 1)
    wait(V, ("dpl", 16))
    V.quantize_mx(T.win[:, 0:POOL], T.wins[:, 0:POOL], T.plt[:, :]).then_inc(S.plq, 1)

    away, near, _, _ = _roads(T, topo, me)
    picks = [(m[0], len(m), "sndp", "pkb%d" % k) for k, m in enumerate(away)]
    picks += [(near[0], 1, "sndp", "pkb3"), (me, 1, "land", "ownb")]
    wait(V, "owna", "plq", "ob", ("arwc", arrive["A"]))
    for r, n, buf, ev in picks:
        V.tensor_copy(T[buf][:, PC * r:PC * (r + n)].bitcast(dt.uint32),
                      T.win[:, :].bitcast(dt.uint32).indirect(T.offb[:, CP * r:CP * (r + n)])).then_inc(S[ev], 1)
    wait(A, "ownas", "plq", "ob", ("arws", arrive["A"]))
    for r, n, buf, ev in picks:
        A.activation(T[buf + "s"][:, PC * r:PC * (r + n)], T.wins[:, :].indirect(T.offb[:, CP * r:CP * (r + n)]),
                     Copy).then_inc(S[ev.replace("pkb", "pkbs").replace("ownb", "ownbs")], 1)
    plan = _plan(T, topo, me, "B")
    need = ((0,), (1, 2, 3))
    for k, call in enumerate(plan):
        wait(g, *["pkb%d" % i for i in need[k]])
        send(call, T.sndp, T.land, PC, PC * me, True, "arpc")
    for k, call in enumerate(plan):
        wait(g, *["pkbs%d" % i for i in need[k]])
        send(call, T.sndps, T.lands, PC, PC * me, False, "arps")
    g.wait_ge(S.left, left[0])

    wait(V, ("dqw", 16))
    V.quantize_mx(T.qwq[:, :], T.qws[:, :], T.qwt[:, :]).then_inc(S.qwd, 1)
    wait(V, "i_p")
    e1 = step(V.tensor_scalar(T.pand[:, 1:2], T.pcol[:, 0:1], 112, None, Op.bitwise_and))
    wait(V, ("dpg", 128))
    e2 = step(V.tensor_copy(T.offg[:, :], T.lpg[:, :]))
    wait(V, e1)
    e3 = step(V.tensor_copy(T.colg[:, :], T.pand[:, 1:2]))
    wait(V, e3, "i_s")
    e4 = step(V.tensor_scalar(T.wslot[:, :], T.cslot[:, :], T.colg[:, 0:1], None, Op.subtract))
    wait(V, e2, e4)
    V.tensor_copy(T.offc[:, :], T.wslot[:, :].indirect(T.offg[:, 0:2])).then_inc(S.oc, 1)

    k = CC // 16
    wait(V, "ownb", "oc", ("arpc", arrive["B"]))
    for c in range(CH):
        V.tensor_copy(T.fin[:, CC * c:CC * c + CC].bitcast(dt.uint32),
                      T.land[:, :].bitcast(dt.uint32).indirect(T.offc[:, k * c:k * c + k])).then_inc(S["fc%d" % c], 1)
    for q in (V, A):
        wait(q, "ownbs", "oc", ("arps", arrive["B"]))
    for c in range(CH):
        a, b = T.fins[:, CC * c:CC * c + CC], T.lands[:, :].indirect(T.offc[:, k * c:k * c + k])
        (A.activation(a, b, Copy) if c % 2 else V.tensor_copy(a, b)).then_inc(S["fs%d" % c], 1)
    wait(P, "qwd")
    half = [(h, o) for h in range(2) for o in range(O)]
    for h, o in half:
        for c in (2 * h, 2 * h + 1):
            if o == 0:
                wait(P, "fc%d" % c, "fs%d" % c)
            b = O * c + o
            P.matmul_mx(T.ps[:, 512 * b:512 * b + CC], T.qwq[:, 128 * o:128 * o + 128], T.qws[:, 128 * o:128 * o + 128],
                        T.fin[:, CC * c:CC * c + CC], T.fins[:, CC * c:CC * c + CC], True, True).then_inc(S["mm%d" % b], 1)
    for h, o in half:
        for c in (2 * h, 2 * h + 1):
            b, at = O * c + o, 512 * o + CC * c
            q = A if c % 2 else V
            wait(q, "mm%d" % b)
            u, v = T.yb[:, at:at + CC], T.ps[:, 512 * b:512 * b + CC]
            (A.activation(u, v, Copy) if c % 2 else V.tensor_copy(u, v)).then_inc(S["cp%d" % b], 1)
            wait(Y, "cp%d" % b)
        at = 512 * o + 2 * CC * h
        Y.dma_start(T.y[:, at:at + 2 * CC], T.yb[:, at:at + 2 * CC]).then_inc(S.ystore, 16)
    Y.wait_ge(S.ystore, 16 * len(half))
